import numpy as np
import ml_dtypes


def mxq(x, axis, fmt="e4m3"):
    dtype, down = {"e4m3": (ml_dtypes.float8_e4m3fn, 7), "e5m2": (ml_dtypes.float8_e5m2, 14)}[fmt]
    v = np.moveaxis(np.asarray(x, np.float32).astype(ml_dtypes.bfloat16).astype(np.float64), axis, -1)
    blocks = v.reshape(v.shape[:-1] + (-1, 32))
    amax = np.abs(blocks).max(-1, keepdims=True)
    byte = np.maximum(np.where(amax > 0, np.frexp(amax)[1] - 1 + 127, 0) - down, 1)
    scale = np.exp2(byte - 127.0)
    codes = (blocks / scale).astype(np.float32).astype(dtype).astype(np.float64)
    return np.moveaxis((codes * scale).reshape(v.shape), -1, axis)


WIDE = False


def mx_kscale(k):
    if not WIDE:
        return np.ones(k)
    levels = np.array([10, -10, 5, -5, 0])
    if k % 512:
        return np.exp2(np.random.permutation(np.resize(levels, k // 32))).repeat(32)
    a = np.empty((k // 512, 16))
    for p in range(k // 512):
        a[p, :8] = np.random.permutation(np.resize(levels, 8))
        for g in range(8):
            far = levels[np.abs(levels - a[p, g]) >= 10]
            a[p, g + 8] = far[np.random.randint(len(far))]
    return np.exp2(a.ravel()).repeat(32)


def f64(x):
    return np.asarray(x).astype(np.float64)


def striped(idx):
    return np.tile(idx.reshape(-1, 16).T, (8, 1)).astype(np.uint16)


def unstriped(offs):
    return offs[:16].T.reshape(-1).astype(np.int64)


def striped8(idx):
    return np.concatenate([x.reshape(-1, 16).T for x in idx]).astype(np.uint16)


def runs(offs, k):
    lists = np.stack([offs[16 * r : 16 * r + 16].T.reshape(-1) for r in range(8)]).astype(np.int64)
    return lists[np.arange(k) % 512 // 64]


def pack_weight(w):
    k, n = w.shape
    w = f64(np.asarray(w, np.float32).astype(ml_dtypes.bfloat16)).reshape(k // 32, 32, n)
    amax = np.abs(w).max(1)
    byte = np.clip(np.where(amax > 0, np.frexp(amax)[1] - 1 + 127 - 7, 1), 1, 254)
    scaled = (w * np.exp2(127.0 - byte)[:, None, :]).reshape(k, n).astype(np.float32)
    words = np.ascontiguousarray(scaled.reshape(k // 512, 128, 4, n).transpose(0, 1, 3, 2)).astype(ml_dtypes.float8_e4m3fn).view(np.uint8)
    return words, np.ascontiguousarray(byte.astype(np.uint8).reshape(k // 512, 16, n))


def unpack_weight(words, scales):
    g, p, n, _ = words.shape
    vals = np.ascontiguousarray(words).view(ml_dtypes.float8_e4m3fn).astype(np.float64) * np.repeat(np.exp2(scales.astype(np.float64) - 127.0), 8, axis=1)[..., None]
    return vals.transpose(0, 1, 3, 2).reshape(g * 512, n)


def sigmoid(v):
    return 1.0 / (1.0 + np.exp(-np.maximum(v, -700.0)))


K, T, S, V, H = 512, 2048, 512, 512, 512


def setup_inputs():
    n = np.random.standard_normal
    s = mx_kscale(K)[:, None]
    u = mx_kscale(S)
    packed_xT = pack_weight(n((K, T)) * s)
    return {
        "x_words": packed_xT[0],
        "x_scales": packed_xT[1],
        "w1": (n((K, H)) / np.sqrt(K) / s).astype(np.float32),
        "w2": (n((K, H)) / np.sqrt(K) / s).astype(np.float32),
        "ga": (np.random.uniform(0.5, 1.5, (H, 1)) * u[:, None]).astype(np.float32),
        "gb": (np.random.uniform(0.5, 1.5, (H, 1)) / u[:, None]).astype(np.float32),
        "offs": striped8(np.random.randint(0, T, (8, S))),
        "two": striped(np.random.permutation(T)[:V]),
        "n1": striped8(np.stack([np.random.permutation(S) for _ in range(8)])),
        "n2": striped8(np.stack([np.random.permutation(S) for _ in range(8)])),
        "n3": striped(np.random.permutation(V)),
        "n4": striped8(np.stack([np.random.permutation(V) for _ in range(8)])),
        "n5": striped8(np.stack([np.random.permutation(V) for _ in range(8)])),
    }


def reference(x_words, x_scales, w1, w2, ga, gb, offs, two, n1, n2, n3, n4, n5):
    xq = unpack_weight(x_words, x_scales)[np.arange(K)[:, None], runs(offs, K)]
    a = mxq(f64(w1), 0, "e4m3").T @ xq
    z = f64(ga) * (a * (sigmoid(a[np.arange(H)[:, None], runs(n1, H)] - (a[np.arange(H)[:, None], runs(n2, H)]))))
    x_two = unpack_weight(x_words, x_scales)[:, unstriped(two)]
    b = mxq(f64(w2), 0, "e4m3").T @ x_two
    z2 = f64(gb) * (b - b[:, unstriped(n3)])
    s = 0.0625 * ((mxq(z, 0, "e4m3").T @ mxq(z2, 0, "e4m3")))
    st = s + 0.5 * (s[np.arange(S)[:, None], runs(n4, S)])
    return st - (st[np.arange(S)[:, None], runs(n5, S)])

@@ -1,0 +1,318 @@
+from contextlib import ExitStack
+
+import concourse.mybir as mybir
+
+F32 = mybir.dt.float32
+BF16 = mybir.dt.bfloat16
+I32 = mybir.dt.int32
+U32 = mybir.dt.uint32
+U16 = mybir.dt.uint16
+U8 = mybir.dt.uint8
+FP8X4 = mybir.dt.float8_e4m3fn_x4
+COPY = mybir.ActivationFunctionType.Copy
+SIGMOID = mybir.ActivationFunctionType.Sigmoid
+ADD = mybir.AluOpType.add
+SUB = mybir.AluOpType.subtract
+MULT = mybir.AluOpType.mult
+
+FLOPS = 3 * 2 * 512 * 512 * 512
+
+P = 128
+PACK = 4
+T = 2048
+N = 512
+HALF = N // 2
+
+
+def tile_picked_hkqcmpdifhop_none_p_kernel(tc, x_words, x_scales, w1, w2, ga, gb, offs, two, n1, n2, n3, n4, n5, out):
+    nc = tc.nc
+    with ExitStack() as ctx:
+        keep = ctx.enter_context(tc.tile_pool(name="keep", bufs=1))
+        reuse = ctx.enter_context(tc.tile_pool(name="reuse", bufs=1))
+        psum = ctx.enter_context(tc.psum_pool(name="psum", bufs=1))
+
+        def load_list(src, name):
+            tile = keep.tile([P, N // 16], U16, name=name)
+            nc.sync.dma_start(tile[:], src)
+            return tile
+
+        scale_table = keep.tile([P, T], U8, name="scale_table")
+        nc.gpsimd.memset(scale_table[:].bitcast(I32), 0)
+        for e in range(2):
+            nc.scalar.dma_start(scale_table[:].bitcast(I32)[e:P:16, :], x_scales[0].bitcast(I32)[e:16:2, :])
+        windows = [keep.tile([P, 2 * N], F32, name=f"window{t}") for t in range(PACK)]
+        for t in range(PACK):
+            nc.vector.memset(windows[t][:, N:], 0.0)
+        hopped = {t: keep.tile([P, 2 * N], F32, name=f"hopped{t}") for t in (0, 2, 3)}
+        for t in (0, 2, 3):
+            nc.vector.memset(hopped[t][:, N:], 0.0)
+        b_rows = keep.tile([P, (PACK + 1) * N], F32, name="b_rows")
+        nc.vector.memset(b_rows[:, PACK * N :], 0.0)
+
+        offs_sb = load_list(offs, "offs_sb")
+        two_sb = load_list(two, "two_sb")
+        n1_sb = load_list(n1, "n1_sb")
+        n2_sb = load_list(n2, "n2_sb")
+        w1_raw = reuse.tile([P, PACK, N], F32, name="w1_raw", offset=4096)
+        nc.sync.dma_start(w1_raw[:], w1.rearrange("(p j) c -> p j c", j=PACK))
+        n3_sb = load_list(n3, "n3_sb")
+        word_table = keep.tile([P, T], U32, name="word_table")
+        nc.sync.dma_start(word_table[:].bitcast(I32), x_words[0].rearrange("p c r -> p (c r)").bitcast(I32))
+        n4_sb = load_list(n4, "n4_sb")
+        n5_sb = load_list(n5, "n5_sb")
+        ga_sb = keep.tile([P, PACK], F32, name="ga_sb")
+        nc.gpsimd.dma_start(ga_sb[:], ga.rearrange("(p t) o -> p (t o)", t=PACK))
+        gb_sb = keep.tile([P, PACK], F32, name="gb_sb")
+        nc.gpsimd.dma_start(gb_sb[:], gb.rearrange("(p t) o -> p (t o)", t=PACK))
+
+        picked_scales = keep.tile([P, 2 * N], U8, name="picked_scales")
+        nc.vector.tensor_copy(picked_scales[:, :N], scale_table[:].indirect(offs_sb[:]))
+        nc.vector.tensor_copy(picked_scales[:, N:], scale_table[:].indirect(two_sb[:]))
+        x_planes = keep.tile([P, 2 * N], U8, name="x_planes", align_bytes=64)
+        nc.vector.tensor_copy(x_planes[:].bitcast(I32), picked_scales[:].bitcast(I32))
+        for e in range(2):
+            nc.sync.dma_start(x_planes[:].bitcast(I32)[2 + e : P : 32, :], picked_scales[:].bitcast(I32)[16 + e : P : 32, :])
+
+        def deal(copy, grouped, planes, t0, t1):
+            copy(
+                grouped[:].rearrange("p (t m j) -> p m j t", t=t1 - t0, j=PACK),
+                planes[:].rearrange("p j (m t) -> p m j t", t=PACK)[:, :, :, t0:t1],
+            )
+
+        def operand(name, width):
+            codes = keep.tile([P, width], U32, name=name + "_codes", align_bytes=64)
+            scales = keep.tile([P, width], U8, name=name + "_scales", align_bytes=64)
+            return codes, scales
+
+        def quantize(q, cols, grouped):
+            nc.vector.quantize_mx(out=q[0][:, cols].bitcast(FP8X4), scales=q[1][:, cols], in_=grouped[:])
+
+        def product(bank, cols, lhs, t, rhs_codes, rhs_scales):
+            rows = slice(t * P, (t + 1) * P)
+            nc.tensor.matmul_mx(
+                out=bank[:, cols],
+                lhsT=lhs[0][:, rows].bitcast(FP8X4),
+                lhsT_scale=lhs[1][:, rows],
+                rhs=rhs_codes.bitcast(FP8X4),
+                rhs_scale=rhs_scales,
+                start=True,
+                stop=True,
+            )
+
+        w1_q = operand("w1", N)
+        w1_grouped = [reuse.tile([P, 2 * N], BF16, name=f"w1_grouped{u}", offset=2048 * u, align_bytes=64) for u in range(2)]
+        for u in range(2):
+            deal(nc.scalar.copy, w1_grouped[u], w1_raw, 2 * u, 2 * u + 2)
+        w2_raw = reuse.tile([P, PACK, N], F32, name="w2_raw", offset=4096)
+        nc.sync.dma_start(w2_raw[:], w2.rearrange("(p j) c -> p j c", j=PACK))
+        for u in range(2):
+            quantize(w1_q, slice(u * HALF, (u + 1) * HALF), w1_grouped[u])
+        xa_codes = reuse.tile([P, N], U32, name="xa_codes", offset=0, align_bytes=64)
+        nc.vector.tensor_copy(xa_codes[:], word_table[:].indirect(offs_sb[:]))
+        a_banks = [psum.tile([P, N], F32, name=f"a_bank{t}", tag=f"bank{t}") for t in range(PACK)]
+        for t in range(PACK):
+            product(a_banks[t], slice(0, N), w1_q, t, xa_codes[:], x_planes[:, :N])
+        xb_codes = reuse.tile([P, N], U32, name="xb_codes", offset=2048, align_bytes=64)
+        nc.vector.tensor_copy(xb_codes[:], word_table[:].indirect(two_sb[:]))
+
+        z_planes = reuse.tile([P, PACK, N], BF16, name="z_planes", offset=12288)
+        second = [keep.tile([P, N], F32, name=f"second{t}") for t in range(PACK)]
+        diff = [keep.tile([P, N], F32, name="diff0")] + [reuse.tile([P, N], F32, name=f"diff{t}", offset=2048 + 2048 * t) for t in range(1, PACK)]
+        gate = [keep.tile([P, N], F32, name=f"gate{t}") for t in range(PACK)]
+
+        def a_out(t, copy=nc.scalar.copy):
+            copy(windows[t][:, :N], a_banks[t][:])
+
+        def fetch(on_vector, dst, src):
+            if on_vector:
+                nc.vector.tensor_copy(dst, src)
+            else:
+                nc.scalar.activation(dst, src, COPY)
+
+        def a_second(t, on_vector=False):
+            fetch(on_vector, second[t][:], windows[t][:].indirect(n2_sb[:]))
+
+        def a_diff(t):
+            nc.vector.tensor_tensor(diff[t][:], windows[t][:].indirect(n1_sb[:]), second[t][:], SUB)
+
+        def a_gate(t):
+            nc.scalar.activation(gate[t][:], diff[t][:], SIGMOID)
+
+        def a_z(t):
+            nc.vector.scalar_tensor_tensor(z_planes[:, t, :], windows[t][:, :N], ga_sb[:, t : t + 1], gate[t][:], MULT, MULT)
+
+        def b_out(t, on_vector):
+            rows = b_rows[:, t * N : (t + 1) * N]
+            if on_vector:
+                nc.vector.tensor_scalar(rows, b_banks[t][:], gb_sb[:, t : t + 1], None, MULT)
+            else:
+                nc.scalar.activation(rows, b_banks[t][:], COPY, scale=gb_sb[:, t : t + 1])
+
+        w2_q = operand("w2", N)
+        w2_grouped = reuse.tile([P, PACK * N], BF16, name="w2_grouped", offset=12288, align_bytes=64)
+        b_banks = [psum.tile([P, N], F32, name=f"b_bank{t}", tag=f"bank{PACK + t}") for t in range(PACK)]
+        z_q = operand("z", N)
+        z_grouped = keep.tile([P, PACK * N], BF16, name="z_grouped", align_bytes=64)
+
+        def w2_deal():
+            deal(nc.vector.tensor_copy, w2_grouped, w2_raw, 0, PACK)
+
+        def w2_product():
+            quantize(w2_q, slice(0, N), w2_grouped)
+            for t in reversed(range(PACK)):
+                product(b_banks[t], slice(0, N), w2_q, t, xb_codes[:], x_planes[:, N:])
+
+        def z_deal():
+            deal(nc.vector.tensor_copy, z_grouped, z_planes, 0, PACK)
+
+        def z_quantize():
+            quantize(z_q, slice(0, N), z_grouped)
+
+        pieces = [slice(0, 256), slice(256, 512)]
+        picked = [keep.tile([P, PACK, c.stop - c.start], F32, name=f"b_picked{h}") for h, c in enumerate(pieces)]
+        z2_grouped = [keep.tile([P, PACK * (c.stop - c.start)], BF16, name=f"z2_grouped{h}", align_bytes=64) for h, c in enumerate(pieces)]
+        z2_q = operand("z2", N)
+        s_banks = {}
+
+        def b_fetch(h, t, on_vector=False):
+            c = pieces[h]
+            fetch(on_vector, picked[h][:, t, :], b_rows[:, t * N : (t + 2) * N].indirect(n3_sb[:, c.start // 16 : c.stop // 16]))
+
+        def b_diff(h):
+            nc.vector.tensor_tensor(
+                z2_grouped[h][:].rearrange("p (c i t) -> p c t i", i=4, t=PACK),
+                b_rows[:, : PACK * N].rearrange("p (t v) -> p t v", t=PACK)[:, :, pieces[h]].rearrange("p t (c i) -> p c t i", i=4),
+                picked[h][:].rearrange("p t (c i) -> p c t i", i=4),
+                SUB,
+            )
+
+        def z2_quantize(h):
+            quantize(z2_q, pieces[h], z2_grouped[h])
+
+        def s_product(h):
+            c = pieces[h]
+            half = c.start // HALF
+            for t in range(PACK):
+                if (half, t) not in s_banks:
+                    s_banks[half, t] = psum.tile([P, HALF], F32, name=f"s_bank{half}{t}", tag=f"bank{PACK * half + t}")
+                product(s_banks[half, t], slice(c.start % HALF, (c.stop - 1) % HALF + 1), z_q, t, z2_q[0][:, c], z2_q[1][:, c])
+
+        a_out(0)
+        a_second(0)
+        a_out(1, nc.vector.tensor_copy)
+        a_second(1, True)
+        a_diff(0)
+        w2_deal()
+        w2_product()
+        a_out(2)
+        a_second(2)
+        a_out(3)
+        a_second(3)
+        a_gate(0)
+        a_diff(1)
+        a_diff(2)
+        a_gate(1)
+        b_out(3, False)
+        a_z(0)
+        a_diff(3)
+        b_out(2, False)
+        a_gate(2)
+        a_z(1)
+        b_out(1, False)
+        b_out(0, True)
+        a_gate(3)
+        a_z(2)
+        a_z(3)
+        z_deal()
+        z_quantize()
+        for t in (3, 2, 1, 0): b_fetch(0, t)
+        b_diff(0)
+        for t in (3, 2, 1, 0): b_fetch(1, t)
+        z2_quantize(0)
+        s_product(0)
+        b_diff(1)
+        z2_quantize(1)
+        s_product(1)
+
+        out_rows = out.rearrange("(p t) v -> p t v", t=PACK)
+        plain = [keep.tile([P, N], F32, name=f"plain{t}") for t in range(PACK)]
+        hop = [keep.tile([P, N], F32, name=f"hop{t}") for t in range(PACK)]
+        hop2 = [keep.tile([P, N], F32, name=f"hop_two{t}") for t in range(PACK)]
+        result = [keep.tile([P, N], F32, name=f"result{t}") for t in range(PACK)]
+
+        def s_out(h, t, on_vector=False):
+            if on_vector:
+                nc.vector.tensor_scalar(windows[t][:, h * HALF : (h + 1) * HALF], s_banks[h, t][:], 0.03125, None, MULT)
+            else:
+                nc.scalar.activation(windows[t][:, h * HALF : (h + 1) * HALF], s_banks[h, t][:], COPY, scale=0.03125)
+
+        def s_double(h, t):
+            c = slice(h * HALF, (h + 1) * HALF)
+            nc.vector.tensor_scalar(plain[t][:, c], windows[t][:, c], 2.0, None, MULT)
+
+        def s_plain(h, t, on_vector=False):
+            if on_vector:
+                nc.vector.tensor_scalar(plain[t][:, h * HALF : (h + 1) * HALF], s_banks[h, t][:], 0.0625, None, MULT)
+            else:
+                nc.scalar.activation(plain[t][:, h * HALF : (h + 1) * HALF], s_banks[h, t][:], COPY, scale=0.0625)
+
+        def fused_plain(t):
+            nc.vector.tensor_scalar(plain[t][:], windows[t][:, :N], 2.0, None, MULT)
+
+        def fused_first(t):
+            nc.vector.tensor_tensor(hop[t][:], windows[t][:].indirect(n4_sb[:]), plain[t][:], ADD)
+
+        def first_hop(t):
+            nc.vector.tensor_tensor(hopped[t][:, :N], windows[t][:].indirect(n4_sb[:]), plain[t][:], ADD)
+
+        def second_fetch(t, c=slice(0, N), on_vector=False):
+            fetch(on_vector, hop2[t][:, c], hopped[t][:].indirect(n5_sb[:, c.start // 16 : c.stop // 16]))
+
+        def second_hop(t, c=slice(0, N)):
+            nc.vector.tensor_tensor(result[t][:, c], hopped[t][:, c], hop2[t][:, c], SUB)
+            nc.sync.dma_start(out_rows[:, t, c], result[t][:, c])
+
+        def fused_negate(t):
+            nc.vector.tensor_scalar(windows[t][:, :N], hop[t][:], -1.0, None, MULT)
+
+        def fused_second(t):
+            nc.vector.tensor_tensor(result[t][:], windows[t][:].indirect(n5_sb[:]), hop[t][:], ADD)
+            nc.sync.dma_start(out_rows[:, t, :], result[t][:])
+
+        def fetch_first(t):
+            nc.scalar.activation(hop[t][:], windows[t][:].indirect(n4_sb[:]), COPY)
+
+        def add_first(t):
+            nc.vector.scalar_tensor_tensor(windows[t][:, :N], windows[t][:, :N], 2.0, hop[t][:], MULT, ADD)
+
+        def fetch_second(t):
+            nc.scalar.activation(hop2[t][:], windows[t][:].indirect(n5_sb[:]), COPY)
+
+        def add_second(t):
+            nc.vector.tensor_tensor(result[t][:], windows[t][:, :N], hop2[t][:], SUB)
+            nc.sync.dma_start(out_rows[:, t, :], result[t][:])
+
+        for t in range(4): s_out(0, t)
+        s_plain(0, 0)
+        s_plain(0, 2, True)
+        s_plain(0, 3, True)
+        s_out(1, 0)
+        s_double(1, 0)
+        s_out(1, 1)
+        first_hop(0)
+        fetch_first(1)
+        s_out(1, 2)
+        s_double(1, 2)
+        s_out(1, 3)
+        first_hop(2)
+        second_fetch(0)
+        add_first(1)
+        s_double(1, 3)
+        second_hop(0)
+        first_hop(3)
+        second_fetch(2)
+        fetch_second(1)
+        second_hop(2)
+        second_fetch(3)
+        add_second(1)
+        second_hop(3)

@@ -36,42 +36,53 @@ def tile_picked_hkqcmpdifhop_none_p_kernel(tc, x_words, x_scales, w1, w2, ga, gb
             nc.sync.dma_start(tile[:], src)
             return tile
 
-        scale_table = keep.tile([P, T], U8, name="scale_table")
-        nc.gpsimd.memset(scale_table[:].bitcast(I32), 0)
-        for e in range(2):
-            nc.scalar.dma_start(scale_table[:].bitcast(I32)[e:P:16, :], x_scales[0].bitcast(I32)[e:16:2, :])
+        scale_table = reuse.tile([P, T], U8, name="scale_table", offset=17408)
+        nc.vector.memset(scale_table[:].bitcast(I32), 0)
+        nc.scalar.dma_start(scale_table[:].bitcast(I32)[0:P:8, :], x_scales[0].bitcast(I32))
+        xa_plane = keep.tile([P, N], U8, name="xa_plane", align_bytes=64)
+        nc.vector.memset(xa_plane[:].bitcast(I32), 0)
+        xb_plane = keep.tile([P, N], U8, name="xb_plane", align_bytes=64)
+        nc.vector.memset(xb_plane[:].bitcast(I32), 0)
         windows = [keep.tile([P, 2 * N], F32, name=f"window{t}") for t in range(PACK)]
         for t in range(PACK):
             nc.vector.memset(windows[t][:, N:], 0.0)
+        warm = keep.tile([P, 1], F32, name="warm")
+        nc.scalar.activation(warm[:], windows[0][:, N : N + 1], SIGMOID)
         hopped = {t: keep.tile([P, 2 * N], F32, name=f"hopped{t}") for t in (0, 2, 3)}
-        for t in (0, 2, 3):
-            nc.vector.memset(hopped[t][:, N:], 0.0)
         b_rows = keep.tile([P, (PACK + 1) * N], F32, name="b_rows")
-        nc.vector.memset(b_rows[:, PACK * N :], 0.0)
 
         offs_sb = load_list(offs, "offs_sb")
         two_sb = load_list(two, "two_sb")
-        n1_sb = load_list(n1, "n1_sb")
-        n2_sb = load_list(n2, "n2_sb")
-        w1_raw = reuse.tile([P, PACK, N], F32, name="w1_raw", offset=4096)
-        nc.sync.dma_start(w1_raw[:], w1.rearrange("(p j) c -> p j c", j=PACK))
-        n3_sb = load_list(n3, "n3_sb")
         word_table = keep.tile([P, T], U32, name="word_table")
         nc.sync.dma_start(word_table[:].bitcast(I32), x_words[0].rearrange("p c r -> p (c r)").bitcast(I32))
+        n1_sb = load_list(n1, "n1_sb")
+        n2_sb = load_list(n2, "n2_sb")
+        n3_sb = load_list(n3, "n3_sb")
         n4_sb = load_list(n4, "n4_sb")
-        n5_sb = load_list(n5, "n5_sb")
-        ga_sb = keep.tile([P, PACK], F32, name="ga_sb")
-        nc.gpsimd.dma_start(ga_sb[:], ga.rearrange("(p t) o -> p (t o)", t=PACK))
-        gb_sb = keep.tile([P, PACK], F32, name="gb_sb")
-        nc.gpsimd.dma_start(gb_sb[:], gb.rearrange("(p t) o -> p (t o)", t=PACK))
+        w1_raw = keep.tile([P, PACK, N], F32, name="w1_raw")
+        nc.sync.dma_start(w1_raw[:], w1.rearrange("(p j) c -> p j c", j=PACK))
 
-        picked_scales = keep.tile([P, 2 * N], U8, name="picked_scales")
-        nc.vector.tensor_copy(picked_scales[:, :N], scale_table[:].indirect(offs_sb[:]))
-        nc.vector.tensor_copy(picked_scales[:, N:], scale_table[:].indirect(two_sb[:]))
-        x_planes = keep.tile([P, 2 * N], U8, name="x_planes", align_bytes=64)
-        nc.vector.tensor_copy(x_planes[:].bitcast(I32), picked_scales[:].bitcast(I32))
-        for e in range(2):
-            nc.sync.dma_start(x_planes[:].bitcast(I32)[2 + e : P : 32, :], picked_scales[:].bitcast(I32)[16 + e : P : 32, :])
+        n5_sb = load_list(n5, "n5_sb")
+
+        def pick_scales(picked, offsets, cols, queue):
+            nc.vector.tensor_copy(picked[:], scale_table[:].indirect(offsets[:]))
+            for i in range(4):
+                queue.dma_start(xa_plane[:].bitcast(I32)[i:P:32, :], picked[:].bitcast(I32)[8 * i : P : 32, :])
+
+        xa_picked = reuse.tile([P, N], U8, name="xa_picked", offset=14336)
+        pick_scales(xa_picked, offs_sb, slice(0, N), nc.sync)
+        xb_picked = keep.tile([P, N], U8, name="xb_picked")
+        nc.vector.tensor_copy(xb_picked[:], scale_table[:].indirect(two_sb[:]))
+        w2_raw = reuse.tile([P, PACK, N], F32, name="w2_raw", offset=17408)
+        nc.sync.dma_start(w2_raw[:], w2.rearrange("(p j) c -> p j c", j=PACK))
+        for i in range(4):
+            nc.sync.dma_start(xb_plane[:].bitcast(I32)[i:P:32, :], xb_picked[:].bitcast(I32)[8 * i : P : 32, :])
+        xa_codes = keep.tile([P, N], U32, name="xa_codes", align_bytes=64)
+        nc.vector.tensor_copy(xa_codes[:], word_table[:].indirect(offs_sb[:]))
+        ga_sb = reuse.tile([P, PACK], F32, name="ga_sb", offset=14336)
+        nc.sync.dma_start(ga_sb[:], ga.rearrange("(p t) o -> p (t o)", t=PACK))
+        gb_sb = reuse.tile([P, PACK], F32, name="gb_sb", offset=14368)
+        nc.sync.dma_start(gb_sb[:], gb.rearrange("(p t) o -> p (t o)", t=PACK))
 
         def deal(copy, grouped, planes, t0, t1):
             copy(
@@ -101,24 +112,20 @@ def tile_picked_hkqcmpdifhop_none_p_kernel(tc, x_words, x_scales, w1, w2, ga, gb
 
         w1_q = operand("w1", N)
         w1_grouped = [reuse.tile([P, 2 * N], BF16, name=f"w1_grouped{u}", offset=2048 * u, align_bytes=64) for u in range(2)]
-        for u in range(2):
-            deal(nc.scalar.copy, w1_grouped[u], w1_raw, 2 * u, 2 * u + 2)
-        w2_raw = reuse.tile([P, PACK, N], F32, name="w2_raw", offset=4096)
-        nc.sync.dma_start(w2_raw[:], w2.rearrange("(p j) c -> p j c", j=PACK))
+        deal(nc.scalar.copy, w1_grouped[1], w1_raw, 2, 4)
+        deal(nc.vector.tensor_copy, w1_grouped[0], w1_raw, 0, 2)
         for u in range(2):
             quantize(w1_q, slice(u * HALF, (u + 1) * HALF), w1_grouped[u])
-        xa_codes = reuse.tile([P, N], U32, name="xa_codes", offset=0, align_bytes=64)
-        nc.vector.tensor_copy(xa_codes[:], word_table[:].indirect(offs_sb[:]))
         a_banks = [psum.tile([P, N], F32, name=f"a_bank{t}", tag=f"bank{t}") for t in range(PACK)]
         for t in range(PACK):
-            product(a_banks[t], slice(0, N), w1_q, t, xa_codes[:], x_planes[:, :N])
+            product(a_banks[t], slice(0, N), w1_q, t, xa_codes[:], xa_plane[:])
         xb_codes = reuse.tile([P, N], U32, name="xb_codes", offset=2048, align_bytes=64)
         nc.vector.tensor_copy(xb_codes[:], word_table[:].indirect(two_sb[:]))
 
-        z_planes = reuse.tile([P, PACK, N], BF16, name="z_planes", offset=12288)
+        z_planes = reuse.tile([P, PACK, N], BF16, name="z_planes", offset=10240)
         second = [keep.tile([P, N], F32, name=f"second{t}") for t in range(PACK)]
-        diff = [keep.tile([P, N], F32, name="diff0")] + [reuse.tile([P, N], F32, name=f"diff{t}", offset=2048 + 2048 * t) for t in range(1, PACK)]
-        gate = [keep.tile([P, N], F32, name=f"gate{t}") for t in range(PACK)]
+        diff = [keep.tile([P, N], F32, name=f"diff{t}") for t in range(PACK)]
+        gate = [hopped[t][:, N:] if t in hopped else b_rows[:, PACK * N :] for t in range(PACK)]
 
         def a_out(t, copy=nc.scalar.copy):
             copy(windows[t][:, :N], a_banks[t][:])
@@ -136,10 +143,10 @@ def tile_picked_hkqcmpdifhop_none_p_kernel(tc, x_words, x_scales, w1, w2, ga, gb
             nc.vector.tensor_tensor(diff[t][:], windows[t][:].indirect(n1_sb[:]), second[t][:], SUB)
 
         def a_gate(t):
-            nc.scalar.activation(gate[t][:], diff[t][:], SIGMOID)
+            nc.scalar.activation(gate[t], diff[t][:], SIGMOID)
 
         def a_z(t):
-            nc.vector.scalar_tensor_tensor(z_planes[:, t, :], windows[t][:, :N], ga_sb[:, t : t + 1], gate[t][:], MULT, MULT)
+            nc.vector.scalar_tensor_tensor(z_planes[:, t, :], windows[t][:, :N], ga_sb[:, t : t + 1], gate[t], MULT, MULT)
 
         def b_out(t, on_vector):
             rows = b_rows[:, t * N : (t + 1) * N]
@@ -149,7 +156,7 @@ def tile_picked_hkqcmpdifhop_none_p_kernel(tc, x_words, x_scales, w1, w2, ga, gb
                 nc.scalar.activation(rows, b_banks[t][:], COPY, scale=gb_sb[:, t : t + 1])
 
         w2_q = operand("w2", N)
-        w2_grouped = reuse.tile([P, PACK * N], BF16, name="w2_grouped", offset=12288, align_bytes=64)
+        w2_grouped = reuse.tile([P, PACK * N], BF16, name="w2_grouped", offset=10240, align_bytes=64)
         b_banks = [psum.tile([P, N], F32, name=f"b_bank{t}", tag=f"bank{PACK + t}") for t in range(PACK)]
         z_q = operand("z", N)
         z_grouped = keep.tile([P, PACK * N], BF16, name="z_grouped", align_bytes=64)
@@ -160,7 +167,7 @@ def tile_picked_hkqcmpdifhop_none_p_kernel(tc, x_words, x_scales, w1, w2, ga, gb
         def w2_product():
             quantize(w2_q, slice(0, N), w2_grouped)
             for t in reversed(range(PACK)):
-                product(b_banks[t], slice(0, N), w2_q, t, xb_codes[:], x_planes[:, N:])
+                product(b_banks[t], slice(0, N), w2_q, t, xb_codes[:], xb_plane[:])
 
         def z_deal():
             deal(nc.vector.tensor_copy, z_grouped, z_planes, 0, PACK)
@@ -170,7 +177,7 @@ def tile_picked_hkqcmpdifhop_none_p_kernel(tc, x_words, x_scales, w1, w2, ga, gb
 
         pieces = [slice(0, 256), slice(256, 512)]
         picked = [keep.tile([P, PACK, c.stop - c.start], F32, name=f"b_picked{h}") for h, c in enumerate(pieces)]
-        z2_grouped = [keep.tile([P, PACK * (c.stop - c.start)], BF16, name=f"z2_grouped{h}", align_bytes=64) for h, c in enumerate(pieces)]
+        z2_grouped = [reuse.tile([P, PACK * HALF], BF16, name=f"z2_grouped{h}", offset=10240, align_bytes=64) for h in range(2)]
         z2_q = operand("z2", N)
         s_banks = {}
 
@@ -199,34 +206,34 @@ def tile_picked_hkqcmpdifhop_none_p_kernel(tc, x_words, x_scales, w1, w2, ga, gb
 
         a_out(0)
         a_second(0)
-        a_out(1, nc.vector.tensor_copy)
-        a_second(1, True)
-        a_diff(0)
         w2_deal()
         w2_product()
+        a_out(1)
+        a_second(1)
+        a_diff(0)
         a_out(2)
         a_second(2)
+        a_diff(1)
+        b_out(3, True)
+        b_out(2, True)
+        a_gate(0)
         a_out(3)
         a_second(3)
-        a_gate(0)
-        a_diff(1)
         a_diff(2)
         a_gate(1)
-        b_out(3, False)
         a_z(0)
         a_diff(3)
-        b_out(2, False)
         a_gate(2)
         a_z(1)
         b_out(1, False)
-        b_out(0, True)
+        b_out(0, False)
         a_gate(3)
         a_z(2)
         a_z(3)
         z_deal()
-        z_quantize()
-        for t in (3, 2, 1, 0): b_fetch(0, t)
+        for t in (3, 2, 1, 0): b_fetch(0, t, t == 0)
         b_diff(0)
+        z_quantize()
         for t in (3, 2, 1, 0): b_fetch(1, t)
         z2_quantize(0)
         s_product(0)
@@ -272,6 +279,11 @@ def tile_picked_hkqcmpdifhop_none_p_kernel(tc, x_words, x_scales, w1, w2, ga, gb
             nc.vector.tensor_tensor(result[t][:, c], hopped[t][:, c], hop2[t][:, c], SUB)
             nc.sync.dma_start(out_rows[:, t, c], result[t][:, c])
 
+        def last_half(t, h):
+            c = slice(h * HALF, (h + 1) * HALF)
+            second_fetch(t, c)
+            second_hop(t, c)
+
         def fused_negate(t):
             nc.vector.tensor_scalar(windows[t][:, :N], hop[t][:], -1.0, None, MULT)
 
@@ -313,6 +325,6 @@ def tile_picked_hkqcmpdifhop_none_p_kernel(tc, x_words, x_scales, w1, w2, ga, gb
         second_fetch(2)
         fetch_second(1)
         second_hop(2)
-        second_fetch(3)
         add_second(1)
-        second_hop(3)
+        last_half(3, 0)
+        last_half(3, 1)

@@ -36,13 +36,10 @@ def tile_picked_hkqcmpdifhop_none_p_kernel(tc, x_words, x_scales, w1, w2, ga, gb
             nc.sync.dma_start(tile[:], src)
             return tile
 
-        scale_table = reuse.tile([P, T], U8, name="scale_table", offset=17408)
+        scale_table = keep.tile([P, T], U8, name="scale_table")
         nc.vector.memset(scale_table[:].bitcast(I32), 0)
-        nc.scalar.dma_start(scale_table[:].bitcast(I32)[0:P:8, :], x_scales[0].bitcast(I32))
-        xa_plane = keep.tile([P, N], U8, name="xa_plane", align_bytes=64)
-        nc.vector.memset(xa_plane[:].bitcast(I32), 0)
-        xb_plane = keep.tile([P, N], U8, name="xb_plane", align_bytes=64)
-        nc.vector.memset(xb_plane[:].bitcast(I32), 0)
+        for e in range(2):
+            nc.scalar.dma_start(scale_table[:].bitcast(I32)[e:P:16, :], x_scales[0].bitcast(I32)[e:16:2, :])
         windows = [keep.tile([P, 2 * N], F32, name=f"window{t}") for t in range(PACK)]
         for t in range(PACK):
             nc.vector.memset(windows[t][:, N:], 0.0)
@@ -52,37 +49,28 @@ def tile_picked_hkqcmpdifhop_none_p_kernel(tc, x_words, x_scales, w1, w2, ga, gb
         b_rows = keep.tile([P, (PACK + 1) * N], F32, name="b_rows")
 
         offs_sb = load_list(offs, "offs_sb")
-        two_sb = load_list(two, "two_sb")
-        word_table = keep.tile([P, T], U32, name="word_table")
-        nc.sync.dma_start(word_table[:].bitcast(I32), x_words[0].rearrange("p c r -> p (c r)").bitcast(I32))
         n1_sb = load_list(n1, "n1_sb")
+        w1_raw = reuse.tile([P, PACK, N], F32, name="w1_raw", offset=2048)
+        nc.sync.dma_start(w1_raw[:], w1.rearrange("(p j) c -> p j c", j=PACK))
+        two_sb = load_list(two, "two_sb")
         n2_sb = load_list(n2, "n2_sb")
         n3_sb = load_list(n3, "n3_sb")
+        word_table = keep.tile([P, T], U32, name="word_table")
+        nc.sync.dma_start(word_table[:].bitcast(I32), x_words[0].rearrange("p c r -> p (c r)").bitcast(I32))
         n4_sb = load_list(n4, "n4_sb")
-        w1_raw = keep.tile([P, PACK, N], F32, name="w1_raw")
-        nc.sync.dma_start(w1_raw[:], w1.rearrange("(p j) c -> p j c", j=PACK))
-
         n5_sb = load_list(n5, "n5_sb")
 
-        def pick_scales(picked, offsets, cols, queue):
-            nc.vector.tensor_copy(picked[:], scale_table[:].indirect(offsets[:]))
-            for i in range(4):
-                queue.dma_start(xa_plane[:].bitcast(I32)[i:P:32, :], picked[:].bitcast(I32)[8 * i : P : 32, :])
+        def place_scales(plane, picked):
+            nc.vector.tensor_copy(plane[:].bitcast(I32), picked[:].bitcast(I32))
+            for e in range(2):
+                nc.sync.dma_start(plane[:].bitcast(I32)[2 + e : P : 32, :], picked[:].bitcast(I32)[16 + e : P : 32, :])
 
-        xa_picked = reuse.tile([P, N], U8, name="xa_picked", offset=14336)
-        pick_scales(xa_picked, offs_sb, slice(0, N), nc.sync)
+        xa_picked = keep.tile([P, N], U8, name="xa_picked")
+        nc.vector.tensor_copy(xa_picked[:], scale_table[:].indirect(offs_sb[:]))
+        xa_scales = keep.tile([P, N], U8, name="xa_scales", align_bytes=64)
+        place_scales(xa_scales, xa_picked)
         xb_picked = keep.tile([P, N], U8, name="xb_picked")
         nc.vector.tensor_copy(xb_picked[:], scale_table[:].indirect(two_sb[:]))
-        w2_raw = reuse.tile([P, PACK, N], F32, name="w2_raw", offset=17408)
-        nc.sync.dma_start(w2_raw[:], w2.rearrange("(p j) c -> p j c", j=PACK))
-        for i in range(4):
-            nc.sync.dma_start(xb_plane[:].bitcast(I32)[i:P:32, :], xb_picked[:].bitcast(I32)[8 * i : P : 32, :])
-        xa_codes = keep.tile([P, N], U32, name="xa_codes", align_bytes=64)
-        nc.vector.tensor_copy(xa_codes[:], word_table[:].indirect(offs_sb[:]))
-        ga_sb = reuse.tile([P, PACK], F32, name="ga_sb", offset=14336)
-        nc.sync.dma_start(ga_sb[:], ga.rearrange("(p t) o -> p (t o)", t=PACK))
-        gb_sb = reuse.tile([P, PACK], F32, name="gb_sb", offset=14368)
-        nc.sync.dma_start(gb_sb[:], gb.rearrange("(p t) o -> p (t o)", t=PACK))
 
         def deal(copy, grouped, planes, t0, t1):
             copy(
@@ -111,20 +99,30 @@ def tile_picked_hkqcmpdifhop_none_p_kernel(tc, x_words, x_scales, w1, w2, ga, gb
             )
 
         w1_q = operand("w1", N)
-        w1_grouped = [reuse.tile([P, 2 * N], BF16, name=f"w1_grouped{u}", offset=2048 * u, align_bytes=64) for u in range(2)]
-        deal(nc.scalar.copy, w1_grouped[1], w1_raw, 2, 4)
-        deal(nc.vector.tensor_copy, w1_grouped[0], w1_raw, 0, 2)
+        w1_grouped = [reuse.tile([P, 2 * N], BF16, name=f"w1_grouped{u}", offset=16896 * u, align_bytes=64) for u in range(2)]
+        for u in range(2):
+            deal(nc.scalar.copy, w1_grouped[u], w1_raw, 2 * u, 2 * u + 2)
+        w2_raw = reuse.tile([P, PACK, N], F32, name="w2_raw", offset=2048)
+        nc.sync.dma_start(w2_raw[:], w2.rearrange("(p j) c -> p j c", j=PACK))
         for u in range(2):
             quantize(w1_q, slice(u * HALF, (u + 1) * HALF), w1_grouped[u])
+        xa_codes = reuse.tile([P, N], U32, name="xa_codes", offset=0, align_bytes=64)
+        nc.vector.tensor_copy(xa_codes[:], word_table[:].indirect(offs_sb[:]))
         a_banks = [psum.tile([P, N], F32, name=f"a_bank{t}", tag=f"bank{t}") for t in range(PACK)]
         for t in range(PACK):
-            product(a_banks[t], slice(0, N), w1_q, t, xa_codes[:], xa_plane[:])
-        xb_codes = reuse.tile([P, N], U32, name="xb_codes", offset=2048, align_bytes=64)
+            product(a_banks[t], slice(0, N), w1_q, t, xa_codes[:], xa_scales[:])
+        ga_sb = reuse.tile([P, PACK], F32, name="ga_sb", offset=16896)
+        nc.sync.dma_start(ga_sb[:], ga.rearrange("(p t) o -> p (t o)", t=PACK))
+        gb_sb = reuse.tile([P, PACK], F32, name="gb_sb", offset=16928)
+        nc.sync.dma_start(gb_sb[:], gb.rearrange("(p t) o -> p (t o)", t=PACK))
+        xb_scales = reuse.tile([P, N], U8, name="xb_scales", offset=16960, align_bytes=64)
+        place_scales(xb_scales, xb_picked)
+        xb_codes = reuse.tile([P, N], U32, name="xb_codes", offset=17472, align_bytes=64)
         nc.vector.tensor_copy(xb_codes[:], word_table[:].indirect(two_sb[:]))
 
-        z_planes = reuse.tile([P, PACK, N], BF16, name="z_planes", offset=10240)
+        z_planes = reuse.tile([P, PACK, N], BF16, name="z_planes", offset=12544)
         second = [keep.tile([P, N], F32, name=f"second{t}") for t in range(PACK)]
-        diff = [keep.tile([P, N], F32, name=f"diff{t}") for t in range(PACK)]
+        diff = [keep.tile([P, N], F32, name="diff0")] + [reuse.tile([P, N], F32, name=f"diff{t}", offset=(8448, 10496, 6144)[t - 1]) for t in range(1, PACK)]
         gate = [hopped[t][:, N:] if t in hopped else b_rows[:, PACK * N :] for t in range(PACK)]
 
         def a_out(t, copy=nc.scalar.copy):
@@ -167,7 +165,7 @@ def tile_picked_hkqcmpdifhop_none_p_kernel(tc, x_words, x_scales, w1, w2, ga, gb
         def w2_product():
             quantize(w2_q, slice(0, N), w2_grouped)
             for t in reversed(range(PACK)):
-                product(b_banks[t], slice(0, N), w2_q, t, xb_codes[:], xb_plane[:])
+                product(b_banks[t], slice(0, N), w2_q, t, xb_codes[:], xb_scales[:])
 
         def z_deal():
             deal(nc.vector.tensor_copy, z_grouped, z_planes, 0, PACK)
@@ -177,7 +175,7 @@ def tile_picked_hkqcmpdifhop_none_p_kernel(tc, x_words, x_scales, w1, w2, ga, gb
 
         pieces = [slice(0, 256), slice(256, 512)]
         picked = [keep.tile([P, PACK, c.stop - c.start], F32, name=f"b_picked{h}") for h, c in enumerate(pieces)]
-        z2_grouped = [reuse.tile([P, PACK * HALF], BF16, name=f"z2_grouped{h}", offset=10240, align_bytes=64) for h in range(2)]
+        z2_grouped = [keep.tile([P, PACK * HALF], BF16, name=f"z2_grouped{h}", align_bytes=64) for h in range(2)]
         z2_q = operand("z2", N)
         s_banks = {}
 
@@ -206,34 +204,34 @@ def tile_picked_hkqcmpdifhop_none_p_kernel(tc, x_words, x_scales, w1, w2, ga, gb
 
         a_out(0)
         a_second(0)
+        a_out(1, nc.vector.tensor_copy)
+        a_second(1, True)
+        a_diff(0)
         w2_deal()
         w2_product()
-        a_out(1)
-        a_second(1)
-        a_diff(0)
         a_out(2)
         a_second(2)
-        a_diff(1)
-        b_out(3, True)
-        b_out(2, True)
-        a_gate(0)
         a_out(3)
         a_second(3)
+        a_gate(0)
+        a_diff(1)
         a_diff(2)
         a_gate(1)
+        b_out(3, False)
         a_z(0)
         a_diff(3)
+        b_out(2, False)
         a_gate(2)
         a_z(1)
         b_out(1, False)
-        b_out(0, False)
+        b_out(0, True)
         a_gate(3)
         a_z(2)
         a_z(3)
         z_deal()
-        for t in (3, 2, 1, 0): b_fetch(0, t, t == 0)
-        b_diff(0)
         z_quantize()
+        for t in (3, 2, 1, 0): b_fetch(0, t)
+        b_diff(0)
         for t in (3, 2, 1, 0): b_fetch(1, t)
         z2_quantize(0)
         s_product(0)

@@ -22,35 +22,93 @@ PACK = 4
 T = 2048
 N = 512
 HALF = N // 2
+GROUP = 16
+QUADRANT = 32
+
+SPLIT_TILE = 1
+FUSED_TILES = (0, 2, 3)
+
+KIB = 1024
+AT_FIRST_STAGE = 0
+AT_RAW = 2 * KIB
+AT_W2_STAGE = AT_RAW + 8 * KIB
+AT_DIFFS = AT_W2_STAGE + 4 * KIB + 256
+AT_Z = AT_DIFFS - 512
+AT_SECOND_STAGE = AT_Z + 4 * KIB + 768
+AT_GA = AT_SECOND_STAGE
+AT_GB = AT_GA + 32
+AT_XB_SCALES = AT_GB + 32
+AT_XB_CODES = AT_XB_SCALES + N
 
 
-def tile_picked_hkqcmpdifhop_none_p_kernel(tc, x_words, x_scales, w1, w2, ga, gb, offs, two, n1, n2, n3, n4, n5, out):
+def tile_picked_hkqcmpdifhop_none_p_kernel(
+    tc, x_words, x_scales, w1, w2, ga, gb, offs, two, n1, n2, n3, n4, n5, out
+):
     nc = tc.nc
+    every_column = slice(0, N)
+    halves = (slice(0, HALF), slice(HALF, N))
     with ExitStack() as ctx:
         keep = ctx.enter_context(tc.tile_pool(name="keep", bufs=1))
         reuse = ctx.enter_context(tc.tile_pool(name="reuse", bufs=1))
         psum = ctx.enter_context(tc.psum_pool(name="psum", bufs=1))
 
         def load_list(src, name):
-            tile = keep.tile([P, N // 16], U16, name=name)
+            tile = keep.tile([P, N // GROUP], U16, name=name)
             nc.sync.dma_start(tile[:], src)
             return tile
+
+        def scalar_fetch(dst, src):
+            nc.scalar.activation(dst, src, COPY)
+
+        def scalar_scale(dst, src, factor):
+            nc.scalar.activation(dst, src, COPY, scale=factor)
+
+        def vector_scale(dst, src, factor):
+            nc.vector.tensor_scalar(dst, src, factor, None, MULT)
+
+        def deal(copy, grouped, planes, t0, t1):
+            copy(
+                grouped[:].rearrange("p (t m j) -> p m j t", t=t1 - t0, j=PACK),
+                planes[:].rearrange("p j (m t) -> p m j t", t=PACK)[:, :, :, t0:t1],
+            )
+
+        def mx_operand(name):
+            codes = keep.tile([P, N], U32, name=name + "_codes", align_bytes=64)
+            scales = keep.tile([P, N], U8, name=name + "_scales", align_bytes=64)
+            return codes, scales
+
+        def quantize(operand, cols, grouped):
+            codes, scales = operand
+            nc.vector.quantize_mx(out=codes[:, cols].bitcast(FP8X4), scales=scales[:, cols], in_=grouped[:])
+
+        def product(bank, stationary, t, moving, cols):
+            rows = slice(t * P, (t + 1) * P)
+            nc.tensor.matmul_mx(
+                out=bank[:],
+                lhsT=stationary[0][:, rows].bitcast(FP8X4),
+                lhsT_scale=stationary[1][:, rows],
+                rhs=moving[0][:, cols].bitcast(FP8X4),
+                rhs_scale=moving[1][:, cols],
+                start=True,
+                stop=True,
+            )
 
         scale_table = keep.tile([P, T], U8, name="scale_table")
         nc.vector.memset(scale_table[:].bitcast(I32), 0)
         for e in range(2):
-            nc.scalar.dma_start(scale_table[:].bitcast(I32)[e:P:16, :], x_scales[0].bitcast(I32)[e:16:2, :])
+            nc.scalar.dma_start(scale_table[:].bitcast(I32)[e:P:GROUP, :], x_scales[0].bitcast(I32)[e : N // QUADRANT : 2, :])
+
         windows = [keep.tile([P, 2 * N], F32, name=f"window{t}") for t in range(PACK)]
         for t in range(PACK):
             nc.vector.memset(windows[t][:, N:], 0.0)
-        warm = keep.tile([P, 1], F32, name="warm")
-        nc.scalar.activation(warm[:], windows[0][:, N : N + 1], SIGMOID)
-        hopped = {t: keep.tile([P, 2 * N], F32, name=f"hopped{t}") for t in (0, 2, 3)}
+        unread = keep.tile([P, 1], F32, name="unread")
+        nc.scalar.activation(unread[:], windows[0][:, N : N + 1], SIGMOID)
+        st_windows = {t: keep.tile([P, 2 * N], F32, name=f"st_window{t}") for t in FUSED_TILES}
         b_rows = keep.tile([P, (PACK + 1) * N], F32, name="b_rows")
 
         offs_sb = load_list(offs, "offs_sb")
         n1_sb = load_list(n1, "n1_sb")
-        w1_raw = reuse.tile([P, PACK, N], F32, name="w1_raw", offset=2048)
+        w1_raw = reuse.tile([P, PACK, N], F32, name="w1_raw", offset=AT_RAW)
         nc.sync.dma_start(w1_raw[:], w1.rearrange("(p j) c -> p j c", j=PACK))
         two_sb = load_list(two, "two_sb")
         n2_sb = load_list(n2, "n2_sb")
@@ -63,7 +121,10 @@ def tile_picked_hkqcmpdifhop_none_p_kernel(tc, x_words, x_scales, w1, w2, ga, gb
         def place_scales(plane, picked):
             nc.vector.tensor_copy(plane[:].bitcast(I32), picked[:].bitcast(I32))
             for e in range(2):
-                nc.sync.dma_start(plane[:].bitcast(I32)[2 + e : P : 32, :], picked[:].bitcast(I32)[16 + e : P : 32, :])
+                nc.sync.dma_start(
+                    plane[:].bitcast(I32)[2 + e : P : QUADRANT, :],
+                    picked[:].bitcast(I32)[GROUP + e : P : QUADRANT, :],
+                )
 
         xa_picked = keep.tile([P, N], U8, name="xa_picked")
         nc.vector.tensor_copy(xa_picked[:], scale_table[:].indirect(offs_sb[:]))
@@ -72,257 +133,172 @@ def tile_picked_hkqcmpdifhop_none_p_kernel(tc, x_words, x_scales, w1, w2, ga, gb
         xb_picked = keep.tile([P, N], U8, name="xb_picked")
         nc.vector.tensor_copy(xb_picked[:], scale_table[:].indirect(two_sb[:]))
 
-        def deal(copy, grouped, planes, t0, t1):
-            copy(
-                grouped[:].rearrange("p (t m j) -> p m j t", t=t1 - t0, j=PACK),
-                planes[:].rearrange("p j (m t) -> p m j t", t=PACK)[:, :, :, t0:t1],
-            )
-
-        def operand(name, width):
-            codes = keep.tile([P, width], U32, name=name + "_codes", align_bytes=64)
-            scales = keep.tile([P, width], U8, name=name + "_scales", align_bytes=64)
-            return codes, scales
-
-        def quantize(q, cols, grouped):
-            nc.vector.quantize_mx(out=q[0][:, cols].bitcast(FP8X4), scales=q[1][:, cols], in_=grouped[:])
-
-        def product(bank, cols, lhs, t, rhs_codes, rhs_scales):
-            rows = slice(t * P, (t + 1) * P)
-            nc.tensor.matmul_mx(
-                out=bank[:, cols],
-                lhsT=lhs[0][:, rows].bitcast(FP8X4),
-                lhsT_scale=lhs[1][:, rows],
-                rhs=rhs_codes.bitcast(FP8X4),
-                rhs_scale=rhs_scales,
-                start=True,
-                stop=True,
-            )
-
-        w1_q = operand("w1", N)
-        w1_grouped = [reuse.tile([P, 2 * N], BF16, name=f"w1_grouped{u}", offset=16896 * u, align_bytes=64) for u in range(2)]
+        w1_mx = mx_operand("w1")
+        w1_grouped = [
+            reuse.tile([P, 2 * N], BF16, name=f"w1_grouped{u}", offset=at, align_bytes=64)
+            for u, at in enumerate((AT_FIRST_STAGE, AT_SECOND_STAGE))
+        ]
         for u in range(2):
             deal(nc.scalar.copy, w1_grouped[u], w1_raw, 2 * u, 2 * u + 2)
-        w2_raw = reuse.tile([P, PACK, N], F32, name="w2_raw", offset=2048)
+        w2_raw = reuse.tile([P, PACK, N], F32, name="w2_raw", offset=AT_RAW)
         nc.sync.dma_start(w2_raw[:], w2.rearrange("(p j) c -> p j c", j=PACK))
         for u in range(2):
-            quantize(w1_q, slice(u * HALF, (u + 1) * HALF), w1_grouped[u])
-        xa_codes = reuse.tile([P, N], U32, name="xa_codes", offset=0, align_bytes=64)
+            quantize(w1_mx, halves[u], w1_grouped[u])
+        xa_codes = reuse.tile([P, N], U32, name="xa_codes", offset=AT_FIRST_STAGE, align_bytes=64)
         nc.vector.tensor_copy(xa_codes[:], word_table[:].indirect(offs_sb[:]))
         a_banks = [psum.tile([P, N], F32, name=f"a_bank{t}", tag=f"bank{t}") for t in range(PACK)]
         for t in range(PACK):
-            product(a_banks[t], slice(0, N), w1_q, t, xa_codes[:], xa_scales[:])
-        ga_sb = reuse.tile([P, PACK], F32, name="ga_sb", offset=16896)
+            product(a_banks[t], w1_mx, t, (xa_codes, xa_scales), every_column)
+
+        ga_sb = reuse.tile([P, PACK], F32, name="ga_sb", offset=AT_GA)
         nc.sync.dma_start(ga_sb[:], ga.rearrange("(p t) o -> p (t o)", t=PACK))
-        gb_sb = reuse.tile([P, PACK], F32, name="gb_sb", offset=16928)
+        gb_sb = reuse.tile([P, PACK], F32, name="gb_sb", offset=AT_GB)
         nc.sync.dma_start(gb_sb[:], gb.rearrange("(p t) o -> p (t o)", t=PACK))
-        xb_scales = reuse.tile([P, N], U8, name="xb_scales", offset=16960, align_bytes=64)
+        xb_scales = reuse.tile([P, N], U8, name="xb_scales", offset=AT_XB_SCALES, align_bytes=64)
         place_scales(xb_scales, xb_picked)
-        xb_codes = reuse.tile([P, N], U32, name="xb_codes", offset=17472, align_bytes=64)
+        xb_codes = reuse.tile([P, N], U32, name="xb_codes", offset=AT_XB_CODES, align_bytes=64)
         nc.vector.tensor_copy(xb_codes[:], word_table[:].indirect(two_sb[:]))
 
-        z_planes = reuse.tile([P, PACK, N], BF16, name="z_planes", offset=12544)
-        second = [keep.tile([P, N], F32, name=f"second{t}") for t in range(PACK)]
-        diff = [keep.tile([P, N], F32, name="diff0")] + [reuse.tile([P, N], F32, name=f"diff{t}", offset=(8448, 10496, 6144)[t - 1]) for t in range(1, PACK)]
-        gate = [hopped[t][:, N:] if t in hopped else b_rows[:, PACK * N :] for t in range(PACK)]
+        z_planes = reuse.tile([P, PACK, N], BF16, name="z_planes", offset=AT_Z)
+        a_at_n2 = [keep.tile([P, N], F32, name=f"a_at_n2_{t}") for t in range(PACK)]
+        diffs = [keep.tile([P, N], F32, name="diff0")] + [
+            reuse.tile([P, N], F32, name=f"diff{t}", offset=AT_DIFFS - 2 * KIB * t) for t in range(1, PACK)
+        ]
+        gates = [st_windows[t][:, N:] if t in st_windows else b_rows[:, PACK * N :] for t in range(PACK)]
 
-        def a_out(t, copy=nc.scalar.copy):
+        def a_out(t, copy):
             copy(windows[t][:, :N], a_banks[t][:])
 
-        def fetch(on_vector, dst, src):
-            if on_vector:
-                nc.vector.tensor_copy(dst, src)
-            else:
-                nc.scalar.activation(dst, src, COPY)
-
-        def a_second(t, on_vector=False):
-            fetch(on_vector, second[t][:], windows[t][:].indirect(n2_sb[:]))
+        def a_fetch(t, fetch):
+            fetch(a_at_n2[t][:], windows[t][:].indirect(n2_sb[:]))
 
         def a_diff(t):
-            nc.vector.tensor_tensor(diff[t][:], windows[t][:].indirect(n1_sb[:]), second[t][:], SUB)
+            nc.vector.tensor_tensor(diffs[t][:], windows[t][:].indirect(n1_sb[:]), a_at_n2[t][:], SUB)
 
         def a_gate(t):
-            nc.scalar.activation(gate[t], diff[t][:], SIGMOID)
+            nc.scalar.activation(gates[t], diffs[t][:], SIGMOID)
 
-        def a_z(t):
-            nc.vector.scalar_tensor_tensor(z_planes[:, t, :], windows[t][:, :N], ga_sb[:, t : t + 1], gate[t], MULT, MULT)
+        def z_plane(t):
+            nc.vector.scalar_tensor_tensor(z_planes[:, t, :], windows[t][:, :N], ga_sb[:, t : t + 1], gates[t], MULT, MULT)
 
-        def b_out(t, on_vector):
-            rows = b_rows[:, t * N : (t + 1) * N]
-            if on_vector:
-                nc.vector.tensor_scalar(rows, b_banks[t][:], gb_sb[:, t : t + 1], None, MULT)
-            else:
-                nc.scalar.activation(rows, b_banks[t][:], COPY, scale=gb_sb[:, t : t + 1])
-
-        w2_q = operand("w2", N)
-        w2_grouped = reuse.tile([P, PACK * N], BF16, name="w2_grouped", offset=10240, align_bytes=64)
+        w2_mx = mx_operand("w2")
+        w2_grouped = reuse.tile([P, PACK * N], BF16, name="w2_grouped", offset=AT_W2_STAGE, align_bytes=64)
         b_banks = [psum.tile([P, N], F32, name=f"b_bank{t}", tag=f"bank{PACK + t}") for t in range(PACK)]
-        z_q = operand("z", N)
+        z_mx = mx_operand("z")
         z_grouped = keep.tile([P, PACK * N], BF16, name="z_grouped", align_bytes=64)
-
-        def w2_deal():
-            deal(nc.vector.tensor_copy, w2_grouped, w2_raw, 0, PACK)
-
-        def w2_product():
-            quantize(w2_q, slice(0, N), w2_grouped)
-            for t in reversed(range(PACK)):
-                product(b_banks[t], slice(0, N), w2_q, t, xb_codes[:], xb_scales[:])
-
-        def z_deal():
-            deal(nc.vector.tensor_copy, z_grouped, z_planes, 0, PACK)
-
-        def z_quantize():
-            quantize(z_q, slice(0, N), z_grouped)
-
-        pieces = [slice(0, 256), slice(256, 512)]
-        picked = [keep.tile([P, PACK, c.stop - c.start], F32, name=f"b_picked{h}") for h, c in enumerate(pieces)]
+        b_at_n3 = [keep.tile([P, PACK, HALF], F32, name=f"b_at_n3_{h}") for h in range(2)]
         z2_grouped = [keep.tile([P, PACK * HALF], BF16, name=f"z2_grouped{h}", align_bytes=64) for h in range(2)]
-        z2_q = operand("z2", N)
+        z2_mx = mx_operand("z2")
         s_banks = {}
 
-        def b_fetch(h, t, on_vector=False):
-            c = pieces[h]
-            fetch(on_vector, picked[h][:, t, :], b_rows[:, t * N : (t + 2) * N].indirect(n3_sb[:, c.start // 16 : c.stop // 16]))
+        def b_out(t, scale):
+            scale(b_rows[:, t * N : (t + 1) * N], b_banks[t][:], gb_sb[:, t : t + 1])
+
+        def b_fetch(h):
+            entries = n3_sb[:, h * HALF // GROUP : (h + 1) * HALF // GROUP]
+            for t in reversed(range(PACK)):
+                scalar_fetch(b_at_n3[h][:, t, :], b_rows[:, t * N : (t + 2) * N].indirect(entries))
 
         def b_diff(h):
+            rows = b_rows[:, : PACK * N].rearrange("p (t v) -> p t v", t=PACK)[:, :, halves[h]]
             nc.vector.tensor_tensor(
                 z2_grouped[h][:].rearrange("p (c i t) -> p c t i", i=4, t=PACK),
-                b_rows[:, : PACK * N].rearrange("p (t v) -> p t v", t=PACK)[:, :, pieces[h]].rearrange("p t (c i) -> p c t i", i=4),
-                picked[h][:].rearrange("p t (c i) -> p c t i", i=4),
+                rows.rearrange("p t (c i) -> p c t i", i=4),
+                b_at_n3[h][:].rearrange("p t (c i) -> p c t i", i=4),
                 SUB,
             )
 
-        def z2_quantize(h):
-            quantize(z2_q, pieces[h], z2_grouped[h])
-
         def s_product(h):
-            c = pieces[h]
-            half = c.start // HALF
+            quantize(z2_mx, halves[h], z2_grouped[h])
             for t in range(PACK):
-                if (half, t) not in s_banks:
-                    s_banks[half, t] = psum.tile([P, HALF], F32, name=f"s_bank{half}{t}", tag=f"bank{PACK * half + t}")
-                product(s_banks[half, t], slice(c.start % HALF, (c.stop - 1) % HALF + 1), z_q, t, z2_q[0][:, c], z2_q[1][:, c])
+                s_banks[h, t] = psum.tile([P, HALF], F32, name=f"s_bank{h}{t}", tag=f"bank{PACK * h + t}")
+                product(s_banks[h, t], z_mx, t, z2_mx, halves[h])
 
-        a_out(0)
-        a_second(0)
+        a_out(0, nc.scalar.copy)
+        a_fetch(0, scalar_fetch)
         a_out(1, nc.vector.tensor_copy)
-        a_second(1, True)
+        a_fetch(1, nc.vector.tensor_copy)
         a_diff(0)
-        w2_deal()
-        w2_product()
-        a_out(2)
-        a_second(2)
-        a_out(3)
-        a_second(3)
+        deal(nc.vector.tensor_copy, w2_grouped, w2_raw, 0, PACK)
+        quantize(w2_mx, every_column, w2_grouped)
+        for t in reversed(range(PACK)):
+            product(b_banks[t], w2_mx, t, (xb_codes, xb_scales), every_column)
+        for t in (2, 3):
+            a_out(t, nc.scalar.copy)
+            a_fetch(t, scalar_fetch)
         a_gate(0)
         a_diff(1)
         a_diff(2)
         a_gate(1)
-        b_out(3, False)
-        a_z(0)
+        b_out(3, scalar_scale)
+        z_plane(0)
         a_diff(3)
-        b_out(2, False)
+        b_out(2, scalar_scale)
         a_gate(2)
-        a_z(1)
-        b_out(1, False)
-        b_out(0, True)
+        z_plane(1)
+        b_out(1, scalar_scale)
+        b_out(0, vector_scale)
         a_gate(3)
-        a_z(2)
-        a_z(3)
-        z_deal()
-        z_quantize()
-        for t in (3, 2, 1, 0): b_fetch(0, t)
+        z_plane(2)
+        z_plane(3)
+        deal(nc.vector.tensor_copy, z_grouped, z_planes, 0, PACK)
+        quantize(z_mx, every_column, z_grouped)
+        b_fetch(0)
         b_diff(0)
-        for t in (3, 2, 1, 0): b_fetch(1, t)
-        z2_quantize(0)
+        b_fetch(1)
         s_product(0)
         b_diff(1)
-        z2_quantize(1)
         s_product(1)
 
         out_rows = out.rearrange("(p t) v -> p t v", t=PACK)
-        plain = [keep.tile([P, N], F32, name=f"plain{t}") for t in range(PACK)]
-        hop = [keep.tile([P, N], F32, name=f"hop{t}") for t in range(PACK)]
-        hop2 = [keep.tile([P, N], F32, name=f"hop_two{t}") for t in range(PACK)]
-        result = [keep.tile([P, N], F32, name=f"result{t}") for t in range(PACK)]
+        s_rows = {t: keep.tile([P, N], F32, name=f"s_rows{t}") for t in FUSED_TILES}
+        half_s_at_n4 = keep.tile([P, N], F32, name="half_s_at_n4")
+        st_at_n5 = [keep.tile([P, N], F32, name=f"st_at_n5_{t}") for t in range(PACK)]
+        results = [keep.tile([P, N], F32, name=f"result{t}") for t in range(PACK)]
+        st_home = [st_windows.get(t, windows[t]) for t in range(PACK)]
 
-        def s_out(h, t, on_vector=False):
-            if on_vector:
-                nc.vector.tensor_scalar(windows[t][:, h * HALF : (h + 1) * HALF], s_banks[h, t][:], 0.03125, None, MULT)
-            else:
-                nc.scalar.activation(windows[t][:, h * HALF : (h + 1) * HALF], s_banks[h, t][:], COPY, scale=0.03125)
+        def half_s_out(h, t):
+            scalar_scale(windows[t][:, halves[h]], s_banks[h, t][:], 1.0 / 32)
 
-        def s_double(h, t):
-            c = slice(h * HALF, (h + 1) * HALF)
-            nc.vector.tensor_scalar(plain[t][:, c], windows[t][:, c], 2.0, None, MULT)
+        def s_out(h, t, scale):
+            scale(s_rows[t][:, halves[h]], s_banks[h, t][:], 1.0 / 16)
 
-        def s_plain(h, t, on_vector=False):
-            if on_vector:
-                nc.vector.tensor_scalar(plain[t][:, h * HALF : (h + 1) * HALF], s_banks[h, t][:], 0.0625, None, MULT)
-            else:
-                nc.scalar.activation(plain[t][:, h * HALF : (h + 1) * HALF], s_banks[h, t][:], COPY, scale=0.0625)
+        def s_from_half(h, t):
+            vector_scale(s_rows[t][:, halves[h]], windows[t][:, halves[h]], 2.0)
 
-        def fused_plain(t):
-            nc.vector.tensor_scalar(plain[t][:], windows[t][:, :N], 2.0, None, MULT)
+        def fused_first_hop(t):
+            nc.vector.tensor_tensor(st_windows[t][:, :N], windows[t][:].indirect(n4_sb[:]), s_rows[t][:], ADD)
 
-        def fused_first(t):
-            nc.vector.tensor_tensor(hop[t][:], windows[t][:].indirect(n4_sb[:]), plain[t][:], ADD)
+        def second_fetch(t):
+            scalar_fetch(st_at_n5[t][:], st_home[t][:].indirect(n5_sb[:]))
 
-        def first_hop(t):
-            nc.vector.tensor_tensor(hopped[t][:, :N], windows[t][:].indirect(n4_sb[:]), plain[t][:], ADD)
+        def finish(t):
+            nc.vector.tensor_tensor(results[t][:], st_home[t][:, :N], st_at_n5[t][:], SUB)
+            nc.sync.dma_start(out_rows[:, t, :], results[t][:])
 
-        def second_fetch(t, c=slice(0, N), on_vector=False):
-            fetch(on_vector, hop2[t][:, c], hopped[t][:].indirect(n5_sb[:, c.start // 16 : c.stop // 16]))
-
-        def second_hop(t, c=slice(0, N)):
-            nc.vector.tensor_tensor(result[t][:, c], hopped[t][:, c], hop2[t][:, c], SUB)
-            nc.sync.dma_start(out_rows[:, t, c], result[t][:, c])
-
-        def last_half(t, h):
-            c = slice(h * HALF, (h + 1) * HALF)
-            second_fetch(t, c)
-            second_hop(t, c)
-
-        def fused_negate(t):
-            nc.vector.tensor_scalar(windows[t][:, :N], hop[t][:], -1.0, None, MULT)
-
-        def fused_second(t):
-            nc.vector.tensor_tensor(result[t][:], windows[t][:].indirect(n5_sb[:]), hop[t][:], ADD)
-            nc.sync.dma_start(out_rows[:, t, :], result[t][:])
-
-        def fetch_first(t):
-            nc.scalar.activation(hop[t][:], windows[t][:].indirect(n4_sb[:]), COPY)
-
-        def add_first(t):
-            nc.vector.scalar_tensor_tensor(windows[t][:, :N], windows[t][:, :N], 2.0, hop[t][:], MULT, ADD)
-
-        def fetch_second(t):
-            nc.scalar.activation(hop2[t][:], windows[t][:].indirect(n5_sb[:]), COPY)
-
-        def add_second(t):
-            nc.vector.tensor_tensor(result[t][:], windows[t][:, :N], hop2[t][:], SUB)
-            nc.sync.dma_start(out_rows[:, t, :], result[t][:])
-
-        for t in range(4): s_out(0, t)
-        s_plain(0, 0)
-        s_plain(0, 2, True)
-        s_plain(0, 3, True)
-        s_out(1, 0)
-        s_double(1, 0)
-        s_out(1, 1)
-        first_hop(0)
-        fetch_first(1)
-        s_out(1, 2)
-        s_double(1, 2)
-        s_out(1, 3)
-        first_hop(2)
+        for t in range(PACK):
+            half_s_out(0, t)
+        s_out(0, 0, scalar_scale)
+        s_out(0, 2, vector_scale)
+        s_out(0, 3, vector_scale)
+        split_half_s = windows[SPLIT_TILE][:, :N]
+        half_s_out(1, 0)
+        s_from_half(1, 0)
+        half_s_out(1, SPLIT_TILE)
+        fused_first_hop(0)
+        scalar_fetch(half_s_at_n4[:], windows[SPLIT_TILE][:].indirect(n4_sb[:]))
+        half_s_out(1, 2)
+        s_from_half(1, 2)
+        half_s_out(1, 3)
+        fused_first_hop(2)
         second_fetch(0)
-        add_first(1)
-        s_double(1, 3)
-        second_hop(0)
-        first_hop(3)
+        nc.vector.scalar_tensor_tensor(split_half_s, split_half_s, 2.0, half_s_at_n4[:], MULT, ADD)
+        s_from_half(1, 3)
+        finish(0)
+        fused_first_hop(3)
         second_fetch(2)
-        fetch_second(1)
-        second_hop(2)
-        add_second(1)
-        last_half(3, 0)
-        last_half(3, 1)
+        second_fetch(SPLIT_TILE)
+        finish(2)
+        second_fetch(3)
+        finish(SPLIT_TILE)
+        finish(3)

@@ -101,8 +101,6 @@ def tile_picked_hkqcmpdifhop_none_p_kernel(
         windows = [keep.tile([P, 2 * N], F32, name=f"window{t}") for t in range(PACK)]
         for t in range(PACK):
             nc.vector.memset(windows[t][:, N:], 0.0)
-        unread = keep.tile([P, 1], F32, name="unread")
-        nc.scalar.activation(unread[:], windows[0][:, N : N + 1], SIGMOID)
         st_windows = {t: keep.tile([P, 2 * N], F32, name=f"st_window{t}") for t in FUSED_TILES}
         b_rows = keep.tile([P, (PACK + 1) * N], F32, name="b_rows")
 

from contextlib import ExitStack

import concourse.mybir as mybir

F32 = mybir.dt.float32
BF16 = mybir.dt.bfloat16
I32 = mybir.dt.int32
U32 = mybir.dt.uint32
U16 = mybir.dt.uint16
U8 = mybir.dt.uint8
FP8X4 = mybir.dt.float8_e4m3fn_x4
COPY = mybir.ActivationFunctionType.Copy
SIGMOID = mybir.ActivationFunctionType.Sigmoid
ADD = mybir.AluOpType.add
SUB = mybir.AluOpType.subtract
MULT = mybir.AluOpType.mult

FLOPS = 3 * 2 * 512 * 512 * 512

P = 128
PACK = 4
T = 2048
N = 512
HALF = N // 2
GROUP = 16
QUADRANT = 32

SPLIT_TILE = 1
FUSED_TILES = (0, 2, 3)

KIB = 1024
AT_FIRST_STAGE = 0
AT_RAW = 2 * KIB
AT_W2_STAGE = AT_RAW + 8 * KIB
AT_DIFFS = AT_W2_STAGE + 4 * KIB + 256
AT_Z = AT_DIFFS - 512
AT_SECOND_STAGE = AT_Z + 4 * KIB + 768
AT_GA = AT_SECOND_STAGE
AT_GB = AT_GA + 32
AT_XB_SCALES = AT_GB + 32
AT_XB_CODES = AT_XB_SCALES + N


def tile_picked_hkqcmpdifhop_none_p_kernel(
    tc, x_words, x_scales, w1, w2, ga, gb, offs, two, n1, n2, n3, n4, n5, out
):
    nc = tc.nc
    every_column = slice(0, N)
    halves = (slice(0, HALF), slice(HALF, N))
    with ExitStack() as ctx:
        keep = ctx.enter_context(tc.tile_pool(name="keep", bufs=1))
        reuse = ctx.enter_context(tc.tile_pool(name="reuse", bufs=1))
        psum = ctx.enter_context(tc.psum_pool(name="psum", bufs=1))

        def load_list(src, name):
            tile = keep.tile([P, N // GROUP], U16, name=name)
            nc.sync.dma_start(tile[:], src)
            return tile

        def scalar_fetch(dst, src):
            nc.scalar.activation(dst, src, COPY)

        def scalar_scale(dst, src, factor):
            nc.scalar.activation(dst, src, COPY, scale=factor)

        def vector_scale(dst, src, factor):
            nc.vector.tensor_scalar(dst, src, factor, None, MULT)

        def deal(copy, grouped, planes, t0, t1):
            copy(
                grouped[:].rearrange("p (t m j) -> p m j t", t=t1 - t0, j=PACK),
                planes[:].rearrange("p j (m t) -> p m j t", t=PACK)[:, :, :, t0:t1],
            )

        def mx_operand(name):
            codes = keep.tile([P, N], U32, name=name + "_codes", align_bytes=64)
            scales = keep.tile([P, N], U8, name=name + "_scales", align_bytes=64)
            return codes, scales

        def quantize(operand, cols, grouped):
            codes, scales = operand
            nc.vector.quantize_mx(out=codes[:, cols].bitcast(FP8X4), scales=scales[:, cols], in_=grouped[:])

        def product(bank, stationary, t, moving, cols):
            rows = slice(t * P, (t + 1) * P)
            nc.tensor.matmul_mx(
                out=bank[:],
                lhsT=stationary[0][:, rows].bitcast(FP8X4),
                lhsT_scale=stationary[1][:, rows],
                rhs=moving[0][:, cols].bitcast(FP8X4),
                rhs_scale=moving[1][:, cols],
                start=True,
                stop=True,
            )

        scale_table = keep.tile([P, T], U8, name="scale_table")
        nc.vector.memset(scale_table[:].bitcast(I32), 0)
        for e in range(2):
            nc.scalar.dma_start(scale_table[:].bitcast(I32)[e:P:GROUP, :], x_scales[0].bitcast(I32)[e : N // QUADRANT : 2, :])

        windows = [keep.tile([P, 2 * N], F32, name=f"window{t}") for t in range(PACK)]
        for t in range(PACK):
            nc.vector.memset(windows[t][:, N:], 0.0)
        st_windows = {t: keep.tile([P, 2 * N], F32, name=f"st_window{t}") for t in FUSED_TILES}
        b_rows = keep.tile([P, (PACK + 1) * N], F32, name="b_rows")

        offs_sb = load_list(offs, "offs_sb")
        n1_sb = load_list(n1, "n1_sb")
        w1_raw = reuse.tile([P, PACK, N], F32, name="w1_raw", offset=AT_RAW)
        nc.sync.dma_start(w1_raw[:], w1.rearrange("(p j) c -> p j c", j=PACK))
        two_sb = load_list(two, "two_sb")
        n2_sb = load_list(n2, "n2_sb")
        n3_sb = load_list(n3, "n3_sb")
        word_table = keep.tile([P, T], U32, name="word_table")
        nc.sync.dma_start(word_table[:].bitcast(I32), x_words[0].rearrange("p c r -> p (c r)").bitcast(I32))
        n4_sb = load_list(n4, "n4_sb")
        n5_sb = load_list(n5, "n5_sb")

        def place_scales(plane, picked):
            nc.vector.tensor_copy(plane[:].bitcast(I32), picked[:].bitcast(I32))
            for e in range(2):
                nc.sync.dma_start(
                    plane[:].bitcast(I32)[2 + e : P : QUADRANT, :],
                    picked[:].bitcast(I32)[GROUP + e : P : QUADRANT, :],
                )

        xa_picked = keep.tile([P, N], U8, name="xa_picked")
        nc.vector.tensor_copy(xa_picked[:], scale_table[:].indirect(offs_sb[:]))
        xa_scales = keep.tile([P, N], U8, name="xa_scales", align_bytes=64)
        place_scales(xa_scales, xa_picked)
        xb_picked = keep.tile([P, N], U8, name="xb_picked")
        nc.vector.tensor_copy(xb_picked[:], scale_table[:].indirect(two_sb[:]))

        w1_mx = mx_operand("w1")
        w1_grouped = [
            reuse.tile([P, 2 * N], BF16, name=f"w1_grouped{u}", offset=at, align_bytes=64)
            for u, at in enumerate((AT_FIRST_STAGE, AT_SECOND_STAGE))
        ]
        for u in range(2):
            deal(nc.scalar.copy, w1_grouped[u], w1_raw, 2 * u, 2 * u + 2)
        w2_raw = reuse.tile([P, PACK, N], F32, name="w2_raw", offset=AT_RAW)
        nc.sync.dma_start(w2_raw[:], w2.rearrange("(p j) c -> p j c", j=PACK))
        for u in range(2):
            quantize(w1_mx, halves[u], w1_grouped[u])
        xa_codes = reuse.tile([P, N], U32, name="xa_codes", offset=AT_FIRST_STAGE, align_bytes=64)
        nc.vector.tensor_copy(xa_codes[:], word_table[:].indirect(offs_sb[:]))
        a_banks = [psum.tile([P, N], F32, name=f"a_bank{t}", tag=f"bank{t}") for t in range(PACK)]
        for t in range(PACK):
            product(a_banks[t], w1_mx, t, (xa_codes, xa_scales), every_column)

        ga_sb = reuse.tile([P, PACK], F32, name="ga_sb", offset=AT_GA)
        nc.sync.dma_start(ga_sb[:], ga.rearrange("(p t) o -> p (t o)", t=PACK))
        gb_sb = reuse.tile([P, PACK], F32, name="gb_sb", offset=AT_GB)
        nc.sync.dma_start(gb_sb[:], gb.rearrange("(p t) o -> p (t o)", t=PACK))
        xb_scales = reuse.tile([P, N], U8, name="xb_scales", offset=AT_XB_SCALES, align_bytes=64)
        place_scales(xb_scales, xb_picked)
        xb_codes = reuse.tile([P, N], U32, name="xb_codes", offset=AT_XB_CODES, align_bytes=64)
        nc.vector.tensor_copy(xb_codes[:], word_table[:].indirect(two_sb[:]))

        z_planes = reuse.tile([P, PACK, N], BF16, name="z_planes", offset=AT_Z)
        a_at_n2 = [keep.tile([P, N], F32, name=f"a_at_n2_{t}") for t in range(PACK)]
        diffs = [keep.tile([P, N], F32, name="diff0")] + [
            reuse.tile([P, N], F32, name=f"diff{t}", offset=AT_DIFFS - 2 * KIB * t) for t in range(1, PACK)
        ]
        gates = [st_windows[t][:, N:] if t in st_windows else b_rows[:, PACK * N :] for t in range(PACK)]

        def a_out(t, copy):
            copy(windows[t][:, :N], a_banks[t][:])

        def a_fetch(t, fetch):
            fetch(a_at_n2[t][:], windows[t][:].indirect(n2_sb[:]))

        def a_diff(t):
            nc.vector.tensor_tensor(diffs[t][:], windows[t][:].indirect(n1_sb[:]), a_at_n2[t][:], SUB)

        def a_gate(t):
            nc.scalar.activation(gates[t], diffs[t][:], SIGMOID)

        def z_plane(t):
            nc.vector.scalar_tensor_tensor(z_planes[:, t, :], windows[t][:, :N], ga_sb[:, t : t + 1], gates[t], MULT, MULT)

        w2_mx = mx_operand("w2")
        w2_grouped = reuse.tile([P, PACK * N], BF16, name="w2_grouped", offset=AT_W2_STAGE, align_bytes=64)
        b_banks = [psum.tile([P, N], F32, name=f"b_bank{t}", tag=f"bank{PACK + t}") for t in range(PACK)]
        z_mx = mx_operand("z")
        z_grouped = keep.tile([P, PACK * N], BF16, name="z_grouped", align_bytes=64)
        b_at_n3 = [keep.tile([P, PACK, HALF], F32, name=f"b_at_n3_{h}") for h in range(2)]
        z2_grouped = [keep.tile([P, PACK * HALF], BF16, name=f"z2_grouped{h}", align_bytes=64) for h in range(2)]
        z2_mx = mx_operand("z2")
        s_banks = {}

        def b_out(t, scale):
            scale(b_rows[:, t * N : (t + 1) * N], b_banks[t][:], gb_sb[:, t : t + 1])

        def b_fetch(h):
            entries = n3_sb[:, h * HALF // GROUP : (h + 1) * HALF // GROUP]
            for t in reversed(range(PACK)):
                scalar_fetch(b_at_n3[h][:, t, :], b_rows[:, t * N : (t + 2) * N].indirect(entries))

        def b_diff(h):
            rows = b_rows[:, : PACK * N].rearrange("p (t v) -> p t v", t=PACK)[:, :, halves[h]]
            nc.vector.tensor_tensor(
                z2_grouped[h][:].rearrange("p (c i t) -> p c t i", i=4, t=PACK),
                rows.rearrange("p t (c i) -> p c t i", i=4),
                b_at_n3[h][:].rearrange("p t (c i) -> p c t i", i=4),
                SUB,
            )

        def s_product(h):
            quantize(z2_mx, halves[h], z2_grouped[h])
            for t in range(PACK):
                s_banks[h, t] = psum.tile([P, HALF], F32, name=f"s_bank{h}{t}", tag=f"bank{PACK * h + t}")
                product(s_banks[h, t], z_mx, t, z2_mx, halves[h])

        a_out(0, nc.scalar.copy)
        a_fetch(0, scalar_fetch)
        a_out(1, nc.vector.tensor_copy)
        a_fetch(1, nc.vector.tensor_copy)
        a_diff(0)
        deal(nc.vector.tensor_copy, w2_grouped, w2_raw, 0, PACK)
        quantize(w2_mx, every_column, w2_grouped)
        for t in reversed(range(PACK)):
            product(b_banks[t], w2_mx, t, (xb_codes, xb_scales), every_column)
        for t in (2, 3):
            a_out(t, nc.scalar.copy)
            a_fetch(t, scalar_fetch)
        a_gate(0)
        a_diff(1)
        a_diff(2)
        a_gate(1)
        b_out(3, scalar_scale)
        z_plane(0)
        a_diff(3)
        b_out(2, scalar_scale)
        a_gate(2)
        z_plane(1)
        b_out(1, scalar_scale)
        b_out(0, vector_scale)
        a_gate(3)
        z_plane(2)
        z_plane(3)
        deal(nc.vector.tensor_copy, z_grouped, z_planes, 0, PACK)
        quantize(z_mx, every_column, z_grouped)
        b_fetch(0)
        b_diff(0)
        b_fetch(1)
        s_product(0)
        b_diff(1)
        s_product(1)

        out_rows = out.rearrange("(p t) v -> p t v", t=PACK)
        s_rows = {t: keep.tile([P, N], F32, name=f"s_rows{t}") for t in FUSED_TILES}
        half_s_at_n4 = keep.tile([P, N], F32, name="half_s_at_n4")
        st_at_n5 = [keep.tile([P, N], F32, name=f"st_at_n5_{t}") for t in range(PACK)]
        results = [keep.tile([P, N], F32, name=f"result{t}") for t in range(PACK)]
        st_home = [st_windows.get(t, windows[t]) for t in range(PACK)]

        def half_s_out(h, t):
            scalar_scale(windows[t][:, halves[h]], s_banks[h, t][:], 1.0 / 32)

        def s_out(h, t, scale):
            scale(s_rows[t][:, halves[h]], s_banks[h, t][:], 1.0 / 16)

        def s_from_half(h, t):
            vector_scale(s_rows[t][:, halves[h]], windows[t][:, halves[h]], 2.0)

        def fused_first_hop(t):
            nc.vector.tensor_tensor(st_windows[t][:, :N], windows[t][:].indirect(n4_sb[:]), s_rows[t][:], ADD)

        def second_fetch(t):
            scalar_fetch(st_at_n5[t][:], st_home[t][:].indirect(n5_sb[:]))

        def finish(t):
            nc.vector.tensor_tensor(results[t][:], st_home[t][:, :N], st_at_n5[t][:], SUB)
            nc.sync.dma_start(out_rows[:, t, :], results[t][:])

        for t in range(PACK):
            half_s_out(0, t)
        s_out(0, 0, scalar_scale)
        s_out(0, 2, vector_scale)
        s_out(0, 3, vector_scale)
        split_half_s = windows[SPLIT_TILE][:, :N]
        half_s_out(1, 0)
        s_from_half(1, 0)
        half_s_out(1, SPLIT_TILE)
        fused_first_hop(0)
        scalar_fetch(half_s_at_n4[:], windows[SPLIT_TILE][:].indirect(n4_sb[:]))
        half_s_out(1, 2)
        s_from_half(1, 2)
        half_s_out(1, 3)
        fused_first_hop(2)
        second_fetch(0)
        nc.vector.scalar_tensor_tensor(split_half_s, split_half_s, 2.0, half_s_at_n4[:], MULT, ADD)
        s_from_half(1, 3)
        finish(0)
        fused_first_hop(3)
        second_fetch(2)
        second_fetch(SPLIT_TILE)
        finish(2)
        second_fetch(3)
        finish(SPLIT_TILE)
        finish(3)
